import numpy as np
import ml_dtypes


def mxq(x, axis, fmt="e4m3"):
    dtype, down = {"e4m3": (ml_dtypes.float8_e4m3fn, 7), "e5m2": (ml_dtypes.float8_e5m2, 14)}[fmt]
    v = np.moveaxis(np.asarray(x, np.float32).astype(ml_dtypes.bfloat16).astype(np.float64), axis, -1)
    blocks = v.reshape(v.shape[:-1] + (-1, 32))
    amax = np.abs(blocks).max(-1, keepdims=True)
    byte = np.maximum(np.where(amax > 0, np.frexp(amax)[1] - 1 + 127, 0) - down, 1)
    scale = np.exp2(byte - 127.0)
    codes = (blocks / scale).astype(np.float32).astype(dtype).astype(np.float64)
    return np.moveaxis((codes * scale).reshape(v.shape), -1, axis)


WIDE = False


def mx_kscale(k):
    if not WIDE:
        return np.ones(k)
    levels = np.array([10, -10, 5, -5, 0])
    if k % 512:
        return np.exp2(np.random.permutation(np.resize(levels, k // 32))).repeat(32)
    a = np.empty((k // 512, 16))
    for p in range(k // 512):
        a[p, :8] = np.random.permutation(np.resize(levels, 8))
        for g in range(8):
            far = levels[np.abs(levels - a[p, g]) >= 10]
            a[p, g + 8] = far[np.random.randint(len(far))]
    return np.exp2(a.ravel()).repeat(32)


BF16 = ml_dtypes.bfloat16


def bf(x):
    return np.asarray(x, np.float32).astype(BF16)


def f64(x):
    return np.asarray(x).astype(np.float64)

def planes(Y):
    n, m = Y.shape
    b = f64(bf(Y)).reshape(n // 32, 32, m)
    amax = np.abs(b).max(1)
    byte = np.clip(np.where(amax > 0, np.frexp(amax)[1] - 1 + 127 - 7, 1), 1, 254)
    codes = (b * np.exp2(127.0 - byte)[:, None, :]).reshape(n, m).astype(np.float32).astype(ml_dtypes.float8_e4m3fn).view(np.uint8)
    words = codes.reshape(n // 512, 128, 4, m).transpose(0, 1, 3, 2)
    return np.ascontiguousarray(words), np.ascontiguousarray(byte.astype(np.uint8).reshape(n // 512, 16, m))


M, K, L, N = 1024, 1024, 1024, 1024


def heat_damp(t, lam):
    return t * np.exp(-0.5 * lam)[None, :]


def soft_correspondence(s):
    nrm = np.sqrt(np.sum(s * s, axis=0) + 1e-6)
    return np.abs(s) / nrm[None, :]


def setup_inputs():
    u, v = mx_kscale(K), mx_kscale(L)
    psi = bf(np.random.standard_normal((M, K)) * u[None, :])
    cmap = bf(np.random.standard_normal((K, L)) / np.sqrt(K) / u[:, None] * v[None, :])
    lam = bf(np.random.uniform(0.2, 4.0, (L,)))
    phi = bf(np.random.standard_normal((N, L)) / np.sqrt(L) / v[None, :])
    dist = bf(np.random.uniform(5.0, 60.0, (M, N)))
    return {"psi": psi, "cmap": cmap, "lam": lam, "phi": phi, "dist": dist}


def core(psi, cmap, lam, phi, dist):
    t = mxq(f64(psi), 1, "e4m3") @ mxq(f64(cmap), 0, "e4m3")
    th = heat_damp(t, f64(lam))
    s = mxq(th, 1, "e4m3") @ mxq(f64(phi), 1, "e4m3").T
    pm = soft_correspondence(s)
    e = pm * f64(dist)
    return e


def reference(psi, cmap, lam, phi, dist):
    R_out = core(psi, cmap, lam, phi, dist)
    words, scales = planes(R_out.T)
    return R_out, words, scales

@@ -1,0 +1,328 @@
+from contextlib import ExitStack
+
+import concourse.mybir as mybir
+from concourse.masks import make_identity
+
+M, K, L, N = 1024, 1024, 1024, 1024
+FLOPS = 2 * M * K * L + 2 * M * L * N
+
+F32 = mybir.dt.float32
+BF16 = mybir.dt.bfloat16
+U32 = mybir.dt.uint32
+I32 = mybir.dt.int32
+U8 = mybir.dt.uint8
+X4 = mybir.dt.float8_e4m3fn_x4
+ACT = mybir.ActivationFunctionType
+ALU = mybir.AluOpType
+
+P = 128
+
+
+def tile_heatdampedfunctionalmapsofterror_x1_kernel(tc, psi, cmap, lam, phi, dist, out_0, out_1, out_2):
+    nc = tc.nc
+    with ExitStack() as ctx:
+        keep = ctx.enter_context(tc.tile_pool(name="keep", bufs=1))
+        work = ctx.enter_context(tc.tile_pool(name="work", bufs=2))
+        psum = ctx.enter_context(tc.psum_pool(name="psum", bufs=1))
+        ctx.enter_context(tc.manual_schedule())
+
+        ident = keep.tile([P, P], F32, name="ident")
+        lam_sb = keep.tile([P, 2, 4], BF16, name="lam_sb")
+        damp = keep.tile([P, 2, 4], F32, name="damp")
+        warm = keep.tile([P, 8], F32, name="warm")
+
+        psi_sb = keep.tile([P, 8, K], BF16, name="psi_sb", align_bytes=64)
+        phi_sb = keep.tile([P, 8, L], BF16, name="phi_sb", align_bytes=64)
+        dist_sb = keep.tile([P, 2, 4, N], BF16, name="dist_sb", align_bytes=64)
+        cm_raw = [keep.tile([P, 4, 512], BF16, name="cm_raw%d" % i, align_bytes=64) for i in range(4)]
+        cm_il = [keep.tile([P, 4, 128, 4], BF16, name="cm_il%d" % i, align_bytes=64) for i in range(4)]
+        cm_c = [keep.tile([P, 512], U32, name="cm_c%d" % i, align_bytes=64) for i in range(4)]
+        cm_s = [keep.tile([P, 512], U8, name="cm_s%d" % i, align_bytes=64) for i in range(4)]
+        psi_c = keep.tile([P, 8, 256], U32, name="psi_c", align_bytes=64)
+        psi_s = keep.tile([P, 8, 256], U8, name="psi_s", align_bytes=64)
+        phi_c = keep.tile([P, 8, 256], U32, name="phi_c", align_bytes=64)
+        phi_s = keep.tile([P, 8, 256], U8, name="phi_s", align_bytes=64)
+        th_c = keep.tile([P, 2, M], U32, name="th_c", align_bytes=64)
+        th_s = keep.tile([P, 2, M], U8, name="th_s", align_bytes=64)
+        pl_s = keep.tile([P, 8, 256], U8, name="pl_s", align_bytes=64)
+        acc = keep.tile([P, 8, 2], F32, name="acc")
+        acce = keep.tile([P, 8], F32, name="acce")
+        rn = keep.tile([P, 8], F32, name="rn")
+
+        nc.scalar.dma_start(out=lam_sb[:], in_=lam.rearrange("(g p t) -> p g t", g=2, t=4))
+
+        def load_cm(kk, g):
+            nc.sync.dma_start(
+                out=cm_raw[2 * kk + g][:],
+                in_=cmap[512 * kk:512 * kk + 512, 512 * g:512 * g + 512].rearrange("(p j) l -> p j l", j=4),
+            )
+
+        def load_rows(dst, src, b, n):
+            nc.sync.dma_start(out=dst[:, b:b + n, :], in_=src[P * b:P * (b + n), :].rearrange("(b p) k -> p b k", p=P))
+
+        load_cm(0, 0)
+        load_cm(1, 0)
+        load_rows(psi_sb, psi, 0, 1)
+        load_rows(psi_sb, psi, 1, 1)
+        load_rows(psi_sb, psi, 2, 2)
+        load_rows(psi_sb, psi, 4, 2)
+        load_rows(psi_sb, psi, 6, 2)
+        load_cm(0, 1)
+        load_cm(1, 1)
+        for b in range(0, 8, 2):
+            load_rows(phi_sb, phi, b, 2)
+        dview = dist.rearrange("(q s p) j -> s p q j", q=4, s=2)
+        for st in range(2):
+            nc.sync.dma_start(out=dist_sb[:, st, :, :], in_=dview[st])
+
+        make_identity(nc, ident[:])
+        nc.scalar.activation(out=damp[:], in_=lam_sb[:], func=ACT.Exp, scale=-0.5)
+
+        def il(eng, kk, g, t0, t1):
+            i = 2 * kk + g
+            dst = cm_il[i][:, t0:t1, :, :]
+            src = cm_raw[i].rearrange("p j (m t) -> p t m j", t=4)[:, t0:t1, :, :]
+            if eng == 0:
+                nc.vector.tensor_copy(out=dst, in_=src)
+            else:
+                nc.scalar.copy(out=dst, in_=src)
+
+        def cm_q(kk, g):
+            i = 2 * kk + g
+            nc.vector.quantize_mx(out=cm_c[i][:].bitcast(X4), scales=cm_s[i][:],
+                                  in_=cm_il[i].rearrange("p t m j -> p (t m j)"))
+
+        banks = {}
+        grouped = {}
+
+        def turn(src, key, b):
+            bank = psum.tile([P, 2, 2, P], F32, name="tr", tag="tr", bufs=3)
+            words = src[:, b, :].bitcast(F32)
+            for kk in range(2):
+                for u in range(2):
+                    nc.tensor.transpose(bank[:, kk, u, :], words[:, 256 * kk + u:256 * (kk + 1):2], ident[:])
+            banks[key, b] = bank
+
+        def group(eng, key, b):
+            gr = work.tile([P, 2, P, 4], BF16, name="gr", tag="gr", bufs=4, align_bytes=64)
+            dst = gr.rearrange("p k r t -> p (k r t)").bitcast(F32).rearrange("p (k r u) -> p k r u", k=2, u=2)
+            src = banks[key, b].rearrange("p k u r -> p k r u")
+            if eng == 0:
+                nc.vector.tensor_copy(out=dst, in_=src)
+            else:
+                nc.scalar.copy(out=dst, in_=src)
+            grouped[key, b] = gr
+
+        def quant(codes, scales, key, b):
+            nc.vector.quantize_mx(out=codes[:, b, :].bitcast(X4), scales=scales[:, b, :],
+                                  in_=grouped[key, b].rearrange("p k r t -> p (k r t)"))
+
+        tbank = {}
+        thb = {}
+
+        def st1(g, b):
+            bank = psum.tile([P, 4, P], F32, name="mm", tag="mm", bufs=4)
+            for t in range(4):
+                for kk in range(2):
+                    i = 2 * kk + g
+                    nc.tensor.matmul_mx(
+                        out=bank[:, t, :],
+                        lhsT=cm_c[i][:, P * t:P * t + P].bitcast(X4), lhsT_scale=cm_s[i][:, P * t:P * t + P],
+                        rhs=psi_c[:, b, P * kk:P * kk + P].bitcast(X4), rhs_scale=psi_s[:, b, P * kk:P * kk + P],
+                        start=(kk == 0), stop=(kk == 1))
+            tbank[g, b] = bank
+
+        def th_mul(g, b):
+            c = b // 2
+            if b % 2 == 0:
+                tht = work.tile([P, 2, P, 4], BF16, name="thb", tag="thb", bufs=3, align_bytes=64)
+                thb[g, c] = tht
+            nc.vector.tensor_tensor(
+                out=thb[g, c][:, b % 2, :, :],
+                in0=tbank[g, b].rearrange("p t i -> p i t"),
+                in1=damp[:, g, :].unsqueeze(1).to_broadcast([P, P, 4]),
+                op=ALU.mult)
+
+        def th_q(g, c):
+            nc.vector.quantize_mx(out=th_c[:, g, 256 * c:256 * c + 256].bitcast(X4), scales=th_s[:, g, 256 * c:256 * c + 256],
+                                  in_=thb[g, c].rearrange("p b r t -> p (b r t)"))
+
+        turn(psi_sb, "psi", 0)
+        turn(psi_sb, "psi", 1)
+        il(0, 0, 0, 0, 2)
+        il(1, 0, 0, 2, 4)
+        il(0, 1, 0, 0, 3)
+        cm_q(0, 0)
+        il(1, 1, 0, 3, 4)
+        group(1, "psi", 0)
+        cm_q(1, 0)
+        group(1, "psi", 1)
+        quant(psi_c, psi_s, "psi", 0)
+        quant(psi_c, psi_s, "psi", 1)
+        for c in range(4):
+            if c < 3:
+                for b in (2 * c + 2, 2 * c + 3):
+                    turn(psi_sb, "psi", b)
+                    group(1, "psi", b)
+            st1(0, 2 * c)
+            st1(0, 2 * c + 1)
+            if c == 1:
+                nc.scalar.activation(out=warm[:], in_=damp[:, 0:2, :].rearrange("p g t -> p (g t)"), func=ACT.Abs_reciprocal_sqrt)
+            if c == 2:
+                il(1, 0, 1, 0, 1)
+                il(1, 0, 1, 1, 2)
+            if c == 3:
+                il(1, 0, 1, 2, 3)
+                il(1, 0, 1, 3, 4)
+                il(1, 1, 1, 0, 2)
+            th_mul(0, 2 * c)
+            if c < 3:
+                quant(psi_c, psi_s, "psi", 2 * c + 2)
+            if c == 3:
+                il(0, 1, 1, 2, 4)
+            th_mul(0, 2 * c + 1)
+            if c < 3:
+                quant(psi_c, psi_s, "psi", 2 * c + 3)
+            if c > 0:
+                th_q(0, c - 1)
+        cm_q(0, 1)
+        cm_q(1, 1)
+        th_q(0, 3)
+        for c in range(4):
+            st1(1, 2 * c)
+            st1(1, 2 * c + 1)
+            turn(phi_sb, "phi", c)
+            group(1, "phi", c)
+            th_mul(1, 2 * c)
+            if c > 0:
+                quant(phi_c, phi_s, "phi", c - 1)
+            th_mul(1, 2 * c + 1)
+            if c > 0:
+                th_q(1, c - 1)
+        quant(phi_c, phi_s, "phi", 3)
+        th_q(1, 3)
+
+        sbank = {}
+        a1 = {}
+        abank = {}
+        ev = {}
+        eb = {}
+        ebank = {}
+        pg = {}
+        pc = {}
+
+        def mm(s, h):
+            bank = psum.tile([P, 512], F32, name="mm", tag="mm", bufs=4)
+            for g in range(2):
+                nc.tensor.matmul_mx(
+                    out=bank[:],
+                    lhsT=phi_c[:, s, P * g:P * g + P].bitcast(X4), lhsT_scale=phi_s[:, s, P * g:P * g + P],
+                    rhs=th_c[:, g, 512 * h:512 * h + 512].bitcast(X4), rhs_scale=th_s[:, g, 512 * h:512 * h + 512],
+                    start=(g == 0), stop=(g == 1))
+            sbank[s, h] = bank
+
+        def norm(s):
+            for h in range(2):
+                junk = work.tile([P, 512], BF16, name="junk", tag="junk", bufs=2)
+                nc.scalar.activation(out=junk[:], in_=sbank[s, h][:], func=ACT.Square, accum_out=acc[:, s, h:h + 1])
+                if h == 0:
+                    nc.scalar.activation(out=acce[:, s:s + 1], in_=acc[:, s, 0:1], func=ACT.Copy, bias=1e-6)
+            nc.scalar.activation(out=rn[:, s:s + 1], in_=acc[:, s, 1:2], func=ACT.Abs_reciprocal_sqrt, bias=acce[:, s:s + 1])
+            a = work.tile([P, M], F32, name="a1", tag="a1", bufs=3)
+            for h in range(2):
+                nc.scalar.activation(out=a[:, 512 * h:512 * h + 512], in_=sbank[s, h][:], func=ACT.Abs, scale=rn[:, s:s + 1])
+            a1[s] = a
+
+        def a1_turn(s):
+            for st in range(2):
+                bank = psum.tile([P, 4, P], F32, name="tr", tag="tr", bufs=3)
+                for q in range(4):
+                    ib = 2 * q + st
+                    nc.tensor.transpose(bank[:, q, :], a1[s][:, P * ib:P * ib + P], ident[:])
+                abank[s, st] = bank
+
+        def emul(s, st):
+            if s % 2 == 0 and st == 0:
+                e = work.tile([P, 2, 4, 256], F32, name="ev", tag="ev", bufs=3)
+                ev[s // 2] = e
+            jo = P * (s % 2)
+            nc.vector.tensor_tensor(out=ev[s // 2][:, st, :, jo:jo + P], in0=abank[s, st][:],
+                                    in1=dist_sb[:, st, :, P * s:P * s + P], op=ALU.mult)
+
+        def cast(s):
+            e = work.tile([P, 2, 2, 4, 32, 2], BF16, name="eb", tag="eb", bufs=3, align_bytes=64)
+            jo = P * (s % 2)
+            src = ev[s // 2].rearrange("p s q j -> p (s q) j")[:, :, jo:jo + P].rearrange("p x (w u e) -> p u x w e", u=2, e=2)
+            for u in range(2):
+                nc.gpsimd.tensor_scalar(out=e[:, u, :, :, :, :].rearrange("p s q w e -> p (s q) w e"), in0=src[:, u, :, :, :],
+                                        scalar1=1.0, scalar2=0.0, op0=ALU.mult, op1=ALU.add)
+            eb[s] = e
+
+        def e_turn(s):
+            bank = psum.tile([P, 2, 2, P], F32, name="ew", tag="ew", bufs=1)
+            words = eb[s].rearrange("p u s q w e -> p (u s q w e)").bitcast(F32)
+            for st in range(2):
+                for u in range(2):
+                    o = 256 * u + 128 * st
+                    nc.tensor.transpose(bank[:, st, u, :], words[:, o:o + P], ident[:])
+            ebank[s] = bank
+
+        def e_group(s):
+            gt = work.tile([P, 2, P, 4], BF16, name="pg", tag="pg", bufs=3, align_bytes=64)
+            dst = gt.rearrange("p k r t -> p (k r t)").bitcast(F32).rearrange("p (k r u) -> p k r u", k=2, u=2)
+            nc.vector.tensor_copy(out=dst, in_=ebank[s].rearrange("p k u r -> p k r u"))
+            pg[s] = gt
+
+        o1 = out_1.bitcast(I32)
+
+        def e_quant(s):
+            ct = work.tile([P, 256], U32, name="pc", tag="pc", bufs=3, align_bytes=64)
+            nc.vector.quantize_mx(out=ct[:].bitcast(X4), scales=pl_s[:, s, :], in_=pg[s].rearrange("p k r t -> p (k r t)"))
+            g, w0 = s // 4, 32 * (s % 4)
+            for q in range(4):
+                nc.sync.dma_start(
+                    out=o1[g, w0:w0 + 32, 256 * q:256 * q + 256, :].rearrange("w i o -> w (i o)"),
+                    in_=ct[32 * q:32 * q + 32, :].bitcast(I32))
+
+        o0 = out_0.rearrange("(q s p) j -> s p q j", q=4, s=2)
+
+        def store(pair):
+            for st in range(2):
+                nc.sync.dma_start(out=o0[st][:, :, 256 * pair:256 * pair + 256], in_=ev[pair][:, st, :, :])
+
+        mm(0, 0)
+        mm(1, 0)
+        mm(0, 1)
+        mm(1, 1)
+        norm(0)
+        for b in range(4, 8):
+            turn(phi_sb, "phi", b)
+            group(0, "phi", b)
+            if b > 4:
+                quant(phi_c, phi_s, "phi", b - 1)
+        for s in range(8):
+            a1_turn(s)
+            emul(s, 0)
+            if s == 0:
+                quant(phi_c, phi_s, "phi", 7)
+            if s > 1:
+                e_quant(s - 2)
+            emul(s, 1)
+            cast(s)
+            if s < 6:
+                mm(s + 2, 0)
+                mm(s + 2, 1)
+            if s < 7:
+                norm(s + 1)
+            if s > 0:
+                e_turn(s - 1)
+                e_group(s - 1)
+            if s % 2 == 1:
+                store(s // 2)
+        e_turn(7)
+        e_quant(6)
+        e_group(7)
+        e_quant(7)
+        o2 = out_2.rearrange("g (s q) i -> q (g s) i", q=4).bitcast(I32)
+        for q in range(4):
+            nc.scalar.dma_start(out=o2[:, :, 64 * q:64 * q + 64], in_=pl_s[32 * q:32 * q + 4, :, :].bitcast(I32))

@@ -16,6 +16,13 @@ ACT = mybir.ActivationFunctionType
 ALU = mybir.AluOpType
 
 P = 128
+MM0 = 99
+CQ = {1: 0, 3: 1}
+PT = {1: 0, 4: 1}
+GE = (1, 1, 1, 1, 1, 1, 1, 1)
+ALT = ((0, 1), (0, 3), (0, 5), (1, 1), (1, 3), (1, 5))
+IL = {(0, 0): "0012", (1, 0): "0012", (0, 1): "0012", (1, 1): "0012"}
+DQ = (("t00",), ("t01",), ("t02",), ("t03", "p0"), ("t10",), (), ("t11", "p1"), ("t12", "t13"))
 
 
 def tile_heatdampedfunctionalmapsofterror_x1_kernel(tc, psi, cmap, lam, phi, dist, out_0, out_1, out_2):
@@ -60,11 +67,11 @@ def tile_heatdampedfunctionalmapsofterror_x1_kernel(tc, psi, cmap, lam, phi, dis
         def load_rows(dst, src, b, n):
             nc.sync.dma_start(out=dst[:, b:b + n, :], in_=src[P * b:P * (b + n), :].rearrange("(b p) k -> p b k", p=P))
 
-        load_cm(0, 0)
-        load_cm(1, 0)
         load_rows(psi_sb, psi, 0, 1)
         load_rows(psi_sb, psi, 1, 1)
         load_rows(psi_sb, psi, 2, 2)
+        load_cm(0, 0)
+        load_cm(1, 0)
         load_rows(psi_sb, psi, 4, 2)
         load_rows(psi_sb, psi, 6, 2)
         load_cm(0, 1)
@@ -84,8 +91,10 @@ def tile_heatdampedfunctionalmapsofterror_x1_kernel(tc, psi, cmap, lam, phi, dis
             src = cm_raw[i].rearrange("p j (m t) -> p t m j", t=4)[:, t0:t1, :, :]
             if eng == 0:
                 nc.vector.tensor_copy(out=dst, in_=src)
-            else:
+            elif eng == 1:
                 nc.scalar.copy(out=dst, in_=src)
+            else:
+                nc.gpsimd.tensor_scalar(out=dst, in0=src, scalar1=1.0, scalar2=0.0, op0=ALU.mult, op1=ALU.add)
 
         def cm_q(kk, g):
             i = 2 * kk + g
@@ -96,7 +105,7 @@ def tile_heatdampedfunctionalmapsofterror_x1_kernel(tc, psi, cmap, lam, phi, dis
         grouped = {}
 
         def turn(src, key, b):
-            bank = psum.tile([P, 2, 2, P], F32, name="tr", tag="tr", bufs=3)
+            bank = psum.tile([P, 2, 2, P], F32, name="tr", tag="tr", bufs=2)
             words = src[:, b, :].bitcast(F32)
             for kk in range(2):
                 for u in range(2):
@@ -121,7 +130,7 @@ def tile_heatdampedfunctionalmapsofterror_x1_kernel(tc, psi, cmap, lam, phi, dis
         thb = {}
 
         def st1(g, b):
-            bank = psum.tile([P, 4, P], F32, name="mm", tag="mm", bufs=4)
+            bank = psum.tile([P, 4, P], F32, name="mm", tag="mm", bufs=5)
             for t in range(4):
                 for kk in range(2):
                     i = 2 * kk + g
@@ -135,7 +144,7 @@ def tile_heatdampedfunctionalmapsofterror_x1_kernel(tc, psi, cmap, lam, phi, dis
         def th_mul(g, b):
             c = b // 2
             if b % 2 == 0:
-                tht = work.tile([P, 2, P, 4], BF16, name="thb", tag="thb", bufs=3, align_bytes=64)
+                tht = work.tile([P, 2, P, 4], BF16, name="thb", tag="thb", bufs=8, align_bytes=64)
                 thb[g, c] = tht
             nc.vector.tensor_tensor(
                 out=thb[g, c][:, b % 2, :, :],
@@ -143,64 +152,26 @@ def tile_heatdampedfunctionalmapsofterror_x1_kernel(tc, psi, cmap, lam, phi, dis
                 in1=damp[:, g, :].unsqueeze(1).to_broadcast([P, P, 4]),
                 op=ALU.mult)
 
+        def th_alt(g, b):
+            c = b // 2
+            if b % 2 == 0:
+                tht = work.tile([P, 2, P, 4], BF16, name="thb", tag="thb", bufs=8, align_bytes=64)
+                thb[g, c] = tht
+            tmp = work.tile([P, 4, P], BF16, name="tmp", tag="tmp", bufs=2, align_bytes=64)
+            for t in range(4):
+                nc.scalar.activation(out=tmp[:, t, :], in_=tbank[g, b][:, t, :], func=ACT.Copy, scale=damp[:, g, t:t + 1])
+            nc.gpsimd.tensor_scalar(out=thb[g, c][:, b % 2, :, :], in0=tmp.rearrange("p t i -> p i t"),
+                                    scalar1=1.0, scalar2=0.0, op0=ALU.mult, op1=ALU.add)
+
+        def th(g, b):
+            if (g, b) in ALT:
+                th_alt(g, b)
+            else:
+                th_mul(g, b)
+
         def th_q(g, c):
             nc.vector.quantize_mx(out=th_c[:, g, 256 * c:256 * c + 256].bitcast(X4), scales=th_s[:, g, 256 * c:256 * c + 256],
                                   in_=thb[g, c].rearrange("p b r t -> p (b r t)"))
-
-        turn(psi_sb, "psi", 0)
-        turn(psi_sb, "psi", 1)
-        il(0, 0, 0, 0, 2)
-        il(1, 0, 0, 2, 4)
-        il(0, 1, 0, 0, 3)
-        cm_q(0, 0)
-        il(1, 1, 0, 3, 4)
-        group(1, "psi", 0)
-        cm_q(1, 0)
-        group(1, "psi", 1)
-        quant(psi_c, psi_s, "psi", 0)
-        quant(psi_c, psi_s, "psi", 1)
-        for c in range(4):
-            if c < 3:
-                for b in (2 * c + 2, 2 * c + 3):
-                    turn(psi_sb, "psi", b)
-                    group(1, "psi", b)
-            st1(0, 2 * c)
-            st1(0, 2 * c + 1)
-            if c == 1:
-                nc.scalar.activation(out=warm[:], in_=damp[:, 0:2, :].rearrange("p g t -> p (g t)"), func=ACT.Abs_reciprocal_sqrt)
-            if c == 2:
-                il(1, 0, 1, 0, 1)
-                il(1, 0, 1, 1, 2)
-            if c == 3:
-                il(1, 0, 1, 2, 3)
-                il(1, 0, 1, 3, 4)
-                il(1, 1, 1, 0, 2)
-            th_mul(0, 2 * c)
-            if c < 3:
-                quant(psi_c, psi_s, "psi", 2 * c + 2)
-            if c == 3:
-                il(0, 1, 1, 2, 4)
-            th_mul(0, 2 * c + 1)
-            if c < 3:
-                quant(psi_c, psi_s, "psi", 2 * c + 3)
-            if c > 0:
-                th_q(0, c - 1)
-        cm_q(0, 1)
-        cm_q(1, 1)
-        th_q(0, 3)
-        for c in range(4):
-            st1(1, 2 * c)
-            st1(1, 2 * c + 1)
-            turn(phi_sb, "phi", c)
-            group(1, "phi", c)
-            th_mul(1, 2 * c)
-            if c > 0:
-                quant(phi_c, phi_s, "phi", c - 1)
-            th_mul(1, 2 * c + 1)
-            if c > 0:
-                th_q(1, c - 1)
-        quant(phi_c, phi_s, "phi", 3)
-        th_q(1, 3)
 
         sbank = {}
         a1 = {}
@@ -212,7 +183,7 @@ def tile_heatdampedfunctionalmapsofterror_x1_kernel(tc, psi, cmap, lam, phi, dis
         pc = {}
 
         def mm(s, h):
-            bank = psum.tile([P, 512], F32, name="mm", tag="mm", bufs=4)
+            bank = psum.tile([P, 512], F32, name="mm", tag="mm", bufs=5)
             for g in range(2):
                 nc.tensor.matmul_mx(
                     out=bank[:],
@@ -221,21 +192,25 @@ def tile_heatdampedfunctionalmapsofterror_x1_kernel(tc, psi, cmap, lam, phi, dis
                     start=(g == 0), stop=(g == 1))
             sbank[s, h] = bank
 
-        def norm(s):
-            for h in range(2):
-                junk = work.tile([P, 512], BF16, name="junk", tag="junk", bufs=2)
-                nc.scalar.activation(out=junk[:], in_=sbank[s, h][:], func=ACT.Square, accum_out=acc[:, s, h:h + 1])
-                if h == 0:
-                    nc.scalar.activation(out=acce[:, s:s + 1], in_=acc[:, s, 0:1], func=ACT.Copy, bias=1e-6)
+        def sq(s, h):
+            junk = work.tile([P, 512], BF16, name="junk", tag="junk", bufs=2)
+            nc.scalar.activation(out=junk[:], in_=sbank[s, h][:], func=ACT.Square, accum_out=acc[:, s, h:h + 1])
+
+        def eps(s):
+            nc.vector.tensor_scalar(out=acce[:, s:s + 1], in0=acc[:, s, 0:1], scalar1=1e-6, scalar2=None, op0=ALU.add)
+
+        def rsq(s):
             nc.scalar.activation(out=rn[:, s:s + 1], in_=acc[:, s, 1:2], func=ACT.Abs_reciprocal_sqrt, bias=acce[:, s:s + 1])
-            a = work.tile([P, M], F32, name="a1", tag="a1", bufs=3)
-            for h in range(2):
-                nc.scalar.activation(out=a[:, 512 * h:512 * h + 512], in_=sbank[s, h][:], func=ACT.Abs, scale=rn[:, s:s + 1])
-            a1[s] = a
+
+        def absn(s, h):
+            if h == 0:
+                a = work.tile([P, M], F32, name="a1", tag="a1", bufs=3)
+                a1[s] = a
+            nc.scalar.activation(out=a1[s][:, 512 * h:512 * h + 512], in_=sbank[s, h][:], func=ACT.Abs, scale=rn[:, s:s + 1])
 
         def a1_turn(s):
             for st in range(2):
-                bank = psum.tile([P, 4, P], F32, name="tr", tag="tr", bufs=3)
+                bank = psum.tile([P, 4, P], F32, name="tr", tag="tr", bufs=2)
                 for q in range(4):
                     ib = 2 * q + st
                     nc.tensor.transpose(bank[:, q, :], a1[s][:, P * ib:P * ib + P], ident[:])
@@ -249,80 +224,194 @@ def tile_heatdampedfunctionalmapsofterror_x1_kernel(tc, psi, cmap, lam, phi, dis
             nc.vector.tensor_tensor(out=ev[s // 2][:, st, :, jo:jo + P], in0=abank[s, st][:],
                                     in1=dist_sb[:, st, :, P * s:P * s + P], op=ALU.mult)
 
-        def cast(s):
-            e = work.tile([P, 2, 2, 4, 32, 2], BF16, name="eb", tag="eb", bufs=3, align_bytes=64)
+        def cast(s, eng, st0, st1):
+            if st0 == 0:
+                e = work.tile([P, 2, 2, 4, 32, 2], BF16, name="eb", tag="eb", bufs=3, align_bytes=64)
+                eb[s] = e
             jo = P * (s % 2)
-            src = ev[s // 2].rearrange("p s q j -> p (s q) j")[:, :, jo:jo + P].rearrange("p x (w u e) -> p u x w e", u=2, e=2)
+            n = st1 - st0
+            src = ev[s // 2][:, st0:st1, :, jo:jo + P].rearrange("p s q (w u e) -> p u (s q) w e", u=2, e=2)
             for u in range(2):
-                nc.gpsimd.tensor_scalar(out=e[:, u, :, :, :, :].rearrange("p s q w e -> p (s q) w e"), in0=src[:, u, :, :, :],
-                                        scalar1=1.0, scalar2=0.0, op0=ALU.mult, op1=ALU.add)
-            eb[s] = e
+                dst = eb[s][:, u, st0:st1, :, :, :].rearrange("p s q w e -> p (s q) w e")
+                if eng == 0:
+                    nc.vector.tensor_copy(out=dst, in_=src[:, u, :, :, :])
+                elif eng == 1:
+                    nc.scalar.copy(out=dst, in_=src[:, u, :, :, :])
+                else:
+                    nc.gpsimd.tensor_scalar(out=dst, in0=src[:, u, :, :, :],
+                                            scalar1=1.0, scalar2=0.0, op0=ALU.mult, op1=ALU.add)
 
-        def e_turn(s):
-            bank = psum.tile([P, 2, 2, P], F32, name="ew", tag="ew", bufs=1)
+        def e_turn(s, st):
+            if st == 0:
+                bank = psum.tile([P, 2, 2, P], F32, name="ew", tag="ew", bufs=1)
+                ebank[s] = bank
             words = eb[s].rearrange("p u s q w e -> p (u s q w e)").bitcast(F32)
-            for st in range(2):
-                for u in range(2):
-                    o = 256 * u + 128 * st
-                    nc.tensor.transpose(bank[:, st, u, :], words[:, o:o + P], ident[:])
-            ebank[s] = bank
+            for u in range(2):
+                o = 256 * u + 128 * st
+                nc.tensor.transpose(ebank[s][:, st, u, :], words[:, o:o + P], ident[:])
 
-        def e_group(s):
-            gt = work.tile([P, 2, P, 4], BF16, name="pg", tag="pg", bufs=3, align_bytes=64)
-            dst = gt.rearrange("p k r t -> p (k r t)").bitcast(F32).rearrange("p (k r u) -> p k r u", k=2, u=2)
-            nc.vector.tensor_copy(out=dst, in_=ebank[s].rearrange("p k u r -> p k r u"))
-            pg[s] = gt
+        def e_group(s, eng, st0, st1):
+            if st0 == 0:
+                gt = work.tile([P, 2, P, 4], BF16, name="pg", tag="pg", bufs=3, align_bytes=64)
+                pg[s] = gt
+            dst = pg[s].rearrange("p k r t -> p (k r t)").bitcast(F32).rearrange("p (k r u) -> p k r u", k=2, u=2)[:, st0:st1, :, :]
+            src = ebank[s].rearrange("p k u r -> p k r u")[:, st0:st1, :, :]
+            if eng == 0:
+                nc.vector.tensor_copy(out=dst, in_=src)
+            else:
+                nc.scalar.copy(out=dst, in_=src)
 
         o1 = out_1.bitcast(I32)
 
-        def e_quant(s):
-            ct = work.tile([P, 256], U32, name="pc", tag="pc", bufs=3, align_bytes=64)
-            nc.vector.quantize_mx(out=ct[:].bitcast(X4), scales=pl_s[:, s, :], in_=pg[s].rearrange("p k r t -> p (k r t)"))
+        def e_quant(s, st0, st1):
+            if st0 == 0:
+                ct = work.tile([P, 256], U32, name="pc", tag="pc", bufs=3, align_bytes=64)
+                pc[s] = ct
+            lo, hi = P * st0, P * st1
+            nc.vector.quantize_mx(out=pc[s][:, lo:hi].bitcast(X4), scales=pl_s[:, s, lo:hi],
+                                  in_=pg[s][:, st0:st1, :, :].rearrange("p k r t -> p (k r t)"))
+
+        def store_words(s, eng):
             g, w0 = s // 4, 32 * (s % 4)
             for q in range(4):
-                nc.sync.dma_start(
+                (nc.sync if eng == 0 else nc.scalar).dma_start(
                     out=o1[g, w0:w0 + 32, 256 * q:256 * q + 256, :].rearrange("w i o -> w (i o)"),
-                    in_=ct[32 * q:32 * q + 32, :].bitcast(I32))
+                    in_=pc[s][32 * q:32 * q + 32, :].bitcast(I32))
 
         o0 = out_0.rearrange("(q s p) j -> s p q j", q=4, s=2)
 
-        def store(pair):
-            for st in range(2):
-                nc.sync.dma_start(out=o0[st][:, :, 256 * pair:256 * pair + 256], in_=ev[pair][:, st, :, :])
+        def store(s0, s1, st):
+            jo = P * (s0 % 2)
+            nc.sync.dma_start(out=o0[st][:, :, P * s0:P * s1], in_=ev[s0 // 2][:, st, :, jo:jo + P * (s1 - s0)])
 
+        def ilp(kk, g, t):
+            il(int(IL[kk, g][t]), kk, g, t, t + 1)
+
+        def il_all(kk, g, e):
+            t = 0
+            while t < 4:
+                t1 = t
+                while t1 < 4 and IL[kk, g][t1] == e:
+                    t1 += 1
+                if t1 > t:
+                    il(int(e), kk, g, t, t1)
+                t = max(t1, t + 1)
+
+        for b in range(4):
+            turn(psi_sb, "psi", b)
+            group(GE[b], "psi", b)
+            if b > 0:
+                quant(psi_c, psi_s, "psi", b - 1)
+        nc.scalar.activation(out=warm[:], in_=damp[:].rearrange("p g t -> p (g t)"), func=ACT.Abs_reciprocal_sqrt)
+        quant(psi_c, psi_s, "psi", 3)
+        for kk in range(2):
+            for e in "012":
+                il_all(kk, 0, e)
+            cm_q(kk, 0)
+        for b in range(4, 8):
+            turn(psi_sb, "psi", b)
+            group(GE[b], "psi", b)
+            if b > 4:
+                quant(psi_c, psi_s, "psi", b - 1)
+        quant(psi_c, psi_s, "psi", 7)
+        for g in range(2):
+            for b in range(8):
+                st1(g, b)
+                if g == 0 and b in CQ:
+                    kk = CQ[b]
+                    for e in "012":
+                        il_all(kk, 1, e)
+                    cm_q(kk, 1)
+                if g == 1 and b in PT:
+                    turn(phi_sb, "phi", PT[b])
+                    group(1, "phi", PT[b])
+                th(g, b)
+                if g == 1:
+                    for x in DQ[b]:
+                        if x[0] == "t":
+                            th_q(int(x[1]), int(x[2]))
+                        else:
+                            quant(phi_c, phi_s, "phi", int(x[1]))
+                    if b == MM0:
+                        mm(0, 0)
+                        sq(0, 0)
+                        eps(0)
+        turn(phi_sb, "phi", 2)
+        group(1, "phi", 2)
         mm(0, 0)
         mm(1, 0)
+        sq(0, 0)
+        eps(0)
+        turn(phi_sb, "phi", 3)
+        group(1, "phi", 3)
         mm(0, 1)
         mm(1, 1)
-        norm(0)
-        for b in range(4, 8):
-            turn(phi_sb, "phi", b)
-            group(0, "phi", b)
-            if b > 4:
-                quant(phi_c, phi_s, "phi", b - 1)
+        quant(phi_c, phi_s, "phi", 2)
+        quant(phi_c, phi_s, "phi", 3)
+        sq(0, 1)
+        sq(1, 0)
+        rsq(0)
+        absn(0, 0)
+        absn(0, 1)
+        sq(1, 1)
+        turn(phi_sb, "phi", 4)
+        group(0, "phi", 4)
+        turn(phi_sb, "phi", 5)
+        group(0, "phi", 5)
+        quant(phi_c, phi_s, "phi", 4)
         for s in range(8):
-            a1_turn(s)
-            emul(s, 0)
-            if s == 0:
-                quant(phi_c, phi_s, "phi", 7)
-            if s > 1:
-                e_quant(s - 2)
-            emul(s, 1)
-            cast(s)
+            last = s == 7
             if s < 6:
                 mm(s + 2, 0)
                 mm(s + 2, 1)
+            a1_turn(s)
+            if s < 2:
+                turn(phi_sb, "phi", 6 + s)
             if s < 7:
-                norm(s + 1)
+                eps(s + 1)
+            emul(s, 0)
+            if s < 3:
+                quant(phi_c, phi_s, "phi", 5 + s)
+            if last:
+                cast(7, 1, 0, 1)
+                store(7, 8, 0)
+            emul(s, 1)
+            if not last:
+                cast(s, 2, 0, 2)
+            if s < 2:
+                group(0, "phi", 6 + s)
+            if s > 1:
+                e_quant(s - 2, 0, 2)
+                store_words(s - 2, 0)
             if s > 0:
-                e_turn(s - 1)
-                e_group(s - 1)
-            if s % 2 == 1:
-                store(s // 2)
-        e_turn(7)
-        e_quant(6)
-        e_group(7)
-        e_quant(7)
+                e_turn(s - 1, 0)
+                e_turn(s - 1, 1)
+                e_group(s - 1, 0, 0, 2)
+            if s < 6:
+                sq(s + 2, 0)
+            if s < 7:
+                rsq(s + 1)
+                absn(s + 1, 0)
+                absn(s + 1, 1)
+            if s < 6:
+                sq(s + 2, 1)
+            if s % 2 == 1 and s < 7:
+                store(s - 1, s + 1, 0)
+                store(s - 1, s + 1, 1)
+            if s == 6:
+                store(6, 7, 0)
+                store(6, 7, 1)
+        cast(7, 1, 1, 2)
+        store(7, 8, 1)
+        e_turn(7, 0)
+        e_quant(6, 0, 2)
+        store_words(6, 0)
+        e_turn(7, 1)
+        e_group(7, 0, 0, 1)
+        e_group(7, 1, 1, 2)
+        e_quant(7, 0, 1)
+        e_quant(7, 1, 2)
+        store_words(7, 0)
         o2 = out_2.rearrange("g (s q) i -> q (g s) i", q=4).bitcast(I32)
         for q in range(4):
             nc.scalar.dma_start(out=o2[:, :, 64 * q:64 * q + 64], in_=pl_s[32 * q:32 * q + 4, :, :].bitcast(I32))

@@ -82,6 +82,8 @@ def tile_heatdampedfunctionalmapsofterror_x1_kernel(tc, psi, cmap, lam, phi, dis
         for st in range(2):
             nc.sync.dma_start(out=dist_sb[:, st, :, :], in_=dview[st])
 
+        wz = keep.tile([P, 512], BF16, name="wz", align_bytes=64)
+        nc.vector.memset(wz[:], 0.0)
         make_identity(nc, ident[:])
         nc.scalar.activation(out=damp[:], in_=lam_sb[:], func=ACT.Exp, scale=-0.5)
 
@@ -103,6 +105,11 @@ def tile_heatdampedfunctionalmapsofterror_x1_kernel(tc, psi, cmap, lam, phi, dis
 
         banks = {}
         grouped = {}
+
+        def spin(n):
+            for i in range(n):
+                bank = psum.tile([P, 512], F32, name="mm", tag="mm", bufs=5)
+                nc.tensor.matmul(bank[:], lhsT=wz[:, 0:P], rhs=wz[:], start=True, stop=True)
 
         def turn(src, key, b):
             bank = psum.tile([P, 2, 2, P], F32, name="tr", tag="tr", bufs=2)
@@ -297,8 +304,10 @@ def tile_heatdampedfunctionalmapsofterror_x1_kernel(tc, psi, cmap, lam, phi, dis
                     il(int(e), kk, g, t, t1)
                 t = max(t1, t + 1)
 
+        spin(5)
         for b in range(4):
             turn(psi_sb, "psi", b)
+            spin(1)
             group(GE[b], "psi", b)
             if b > 0:
                 quant(psi_c, psi_s, "psi", b - 1)
@@ -308,8 +317,11 @@ def tile_heatdampedfunctionalmapsofterror_x1_kernel(tc, psi, cmap, lam, phi, dis
             for e in "012":
                 il_all(kk, 0, e)
             cm_q(kk, 0)
+        spin(6)
         for b in range(4, 8):
             turn(psi_sb, "psi", b)
+            if b % 2 == 1:
+                spin(1)
             group(GE[b], "psi", b)
             if b > 4:
                 quant(psi_c, psi_s, "psi", b - 1)
@@ -363,8 +375,9 @@ def tile_heatdampedfunctionalmapsofterror_x1_kernel(tc, psi, cmap, lam, phi, dis
             last = s == 7
             if s < 6:
                 mm(s + 2, 0)
-                mm(s + 2, 1)
             a1_turn(s)
+            if s < 6:
+                mm(s + 2, 1)
             if s < 2:
                 turn(phi_sb, "phi", 6 + s)
             if s < 7:
@@ -372,12 +385,12 @@ def tile_heatdampedfunctionalmapsofterror_x1_kernel(tc, psi, cmap, lam, phi, dis
             emul(s, 0)
             if s < 3:
                 quant(phi_c, phi_s, "phi", 5 + s)
+            cast(s, 1 if last else 2, 0, 1)
             if last:
-                cast(7, 1, 0, 1)
                 store(7, 8, 0)
             emul(s, 1)
             if not last:
-                cast(s, 2, 0, 2)
+                cast(s, 2, 1, 2)
             if s < 2:
                 group(0, "phi", 6 + s)
             if s > 1:

@@ -16,12 +16,13 @@ ACT = mybir.ActivationFunctionType
 ALU = mybir.AluOpType
 
 P = 128
+CE = (2, 0)
 MM0 = 99
 CQ = {1: 0, 3: 1}
 PT = {1: 0, 4: 1}
 GE = (1, 1, 1, 1, 1, 1, 1, 1)
-ALT = ((0, 1), (0, 3), (0, 5), (1, 1), (1, 3), (1, 5))
-IL = {(0, 0): "0012", (1, 0): "0012", (0, 1): "0012", (1, 1): "0012"}
+ALT = ((0, 3), (0, 5), (0, 7), (1, 1), (1, 3), (1, 5))
+IL = {(0, 0): "0011", (1, 0): "0011", (0, 1): "0111", (1, 1): "0111"}
 DQ = (("t00",), ("t01",), ("t02",), ("t03", "p0"), ("t10",), (), ("t11", "p1"), ("t12", "t13"))
 
 
@@ -159,16 +160,20 @@ def tile_heatdampedfunctionalmapsofterror_x1_kernel(tc, psi, cmap, lam, phi, dis
                 in1=damp[:, g, :].unsqueeze(1).to_broadcast([P, P, 4]),
                 op=ALU.mult)
 
+        late = {}
+
         def th_alt(g, b):
             c = b // 2
             if b % 2 == 0:
                 tht = work.tile([P, 2, P, 4], BF16, name="thb", tag="thb", bufs=8, align_bytes=64)
                 thb[g, c] = tht
-            tmp = work.tile([P, 4, P], BF16, name="tmp", tag="tmp", bufs=2, align_bytes=64)
+            tmp = work.tile([P, 4, P], BF16, name="tmp", tag="tmp", bufs=3, align_bytes=64)
             for t in range(4):
                 nc.scalar.activation(out=tmp[:, t, :], in_=tbank[g, b][:, t, :], func=ACT.Copy, scale=damp[:, g, t:t + 1])
-            nc.gpsimd.tensor_scalar(out=thb[g, c][:, b % 2, :, :], in0=tmp.rearrange("p t i -> p i t"),
-                                    scalar1=1.0, scalar2=0.0, op0=ALU.mult, op1=ALU.add)
+            late[g, b] = tmp
+
+        def th_late(g, b):
+            nc.vector.tensor_copy(out=thb[g, b // 2][:, b % 2, :, :], in_=late[g, b].rearrange("p t i -> p i t"))
 
         def th(g, b):
             if (g, b) in ALT:
@@ -224,37 +229,32 @@ def tile_heatdampedfunctionalmapsofterror_x1_kernel(tc, psi, cmap, lam, phi, dis
                 abank[s, st] = bank
 
         def emul(s, st):
-            if s % 2 == 0 and st == 0:
-                e = work.tile([P, 2, 4, 256], F32, name="ev", tag="ev", bufs=3)
-                ev[s // 2] = e
-            jo = P * (s % 2)
-            nc.vector.tensor_tensor(out=ev[s // 2][:, st, :, jo:jo + P], in0=abank[s, st][:],
+            if st == 0:
+                e = work.tile([P, 2, 4, P], F32, name="ev", tag="ev", bufs=4)
+                ev[s] = e
+            nc.vector.tensor_tensor(out=ev[s][:, st, :, :], in0=abank[s, st][:],
                                     in1=dist_sb[:, st, :, P * s:P * s + P], op=ALU.mult)
 
-        def cast(s, eng, st0, st1):
-            if st0 == 0:
-                e = work.tile([P, 2, 2, 4, 32, 2], BF16, name="eb", tag="eb", bufs=3, align_bytes=64)
+        def cast(s, eng, st):
+            if st == 0:
+                e = work.tile([P, 2, 2, P, 2], BF16, name="eb", tag="eb", bufs=4, align_bytes=64)
                 eb[s] = e
-            jo = P * (s % 2)
-            n = st1 - st0
-            src = ev[s // 2][:, st0:st1, :, jo:jo + P].rearrange("p s q (w u e) -> p u (s q) w e", u=2, e=2)
-            for u in range(2):
-                dst = eb[s][:, u, st0:st1, :, :, :].rearrange("p s q w e -> p (s q) w e")
-                if eng == 0:
-                    nc.vector.tensor_copy(out=dst, in_=src[:, u, :, :, :])
-                elif eng == 1:
-                    nc.scalar.copy(out=dst, in_=src[:, u, :, :, :])
-                else:
-                    nc.gpsimd.tensor_scalar(out=dst, in0=src[:, u, :, :, :],
-                                            scalar1=1.0, scalar2=0.0, op0=ALU.mult, op1=ALU.add)
+            src = ev[s][:, st, :, :].rearrange("p q (w u e) -> p (q w) u e", u=2, e=2)
+            dst = eb[s][:, st, :, :, :].rearrange("p u x e -> p x u e")
+            if eng == 0:
+                nc.vector.tensor_copy(out=dst, in_=src)
+            elif eng == 1:
+                nc.scalar.copy(out=dst, in_=src)
+            else:
+                nc.gpsimd.tensor_scalar(out=dst, in0=src, scalar1=1.0, scalar2=0.0, op0=ALU.mult, op1=ALU.add)
 
         def e_turn(s, st):
             if st == 0:
                 bank = psum.tile([P, 2, 2, P], F32, name="ew", tag="ew", bufs=1)
                 ebank[s] = bank
-            words = eb[s].rearrange("p u s q w e -> p (u s q w e)").bitcast(F32)
+            words = eb[s].rearrange("p s u x e -> p (s u x e)").bitcast(F32)
             for u in range(2):
-                o = 256 * u + 128 * st
+                o = 256 * st + 128 * u
                 nc.tensor.transpose(ebank[s][:, st, u, :], words[:, o:o + P], ident[:])
 
         def e_group(s, eng, st0, st1):
@@ -287,9 +287,8 @@ def tile_heatdampedfunctionalmapsofterror_x1_kernel(tc, psi, cmap, lam, phi, dis
 
         o0 = out_0.rearrange("(q s p) j -> s p q j", q=4, s=2)
 
-        def store(s0, s1, st):
-            jo = P * (s0 % 2)
-            nc.sync.dma_start(out=o0[st][:, :, P * s0:P * s1], in_=ev[s0 // 2][:, st, :, jo:jo + P * (s1 - s0)])
+        def store(s, st):
+            nc.sync.dma_start(out=o0[st][:, :, P * s:P * s + P], in_=ev[s][:, st, :, :])
 
         def ilp(kk, g, t):
             il(int(IL[kk, g][t]), kk, g, t, t + 1)
@@ -338,6 +337,10 @@ def tile_heatdampedfunctionalmapsofterror_x1_kernel(tc, psi, cmap, lam, phi, dis
                     turn(phi_sb, "phi", PT[b])
                     group(1, "phi", PT[b])
                 th(g, b)
+                if (g, b - 1) in ALT:
+                    th_late(g, b - 1)
+                elif g == 1 and b == 0 and (0, 7) in ALT:
+                    th_late(0, 7)
                 if g == 1:
                     for x in DQ[b]:
                         if x[0] == "t":
@@ -385,12 +388,11 @@ def tile_heatdampedfunctionalmapsofterror_x1_kernel(tc, psi, cmap, lam, phi, dis
             emul(s, 0)
             if s < 3:
                 quant(phi_c, phi_s, "phi", 5 + s)
-            cast(s, 1 if last else 2, 0, 1)
-            if last:
-                store(7, 8, 0)
+            cast(s, 1 if last else CE[0], 0)
+            store(s, 0)
             emul(s, 1)
-            if not last:
-                cast(s, 2, 1, 2)
+            cast(s, 1 if last else CE[1], 1)
+            store(s, 1)
             if s < 2:
                 group(0, "phi", 6 + s)
             if s > 1:
@@ -408,14 +410,6 @@ def tile_heatdampedfunctionalmapsofterror_x1_kernel(tc, psi, cmap, lam, phi, dis
                 absn(s + 1, 1)
             if s < 6:
                 sq(s + 2, 1)
-            if s % 2 == 1 and s < 7:
-                store(s - 1, s + 1, 0)
-                store(s - 1, s + 1, 1)
-            if s == 6:
-                store(6, 7, 0)
-                store(6, 7, 1)
-        cast(7, 1, 1, 2)
-        store(7, 8, 1)
         e_turn(7, 0)
         e_quant(6, 0, 2)
         store_words(6, 0)

@@ -16,14 +16,21 @@ ACT = mybir.ActivationFunctionType
 ALU = mybir.AluOpType
 
 P = 128
+EM = (6, 7)
+PG = (0, 0, 0, 0)
+EG = (0, 0, 0, 0, 0, 0, 0)
+SPREAD = True
+CMQ = (3, 4)
+ILS = ((), (), ((1, 0, 2, 4), (0, 1, 0, 1)), ((1, 1, 1, 2), (0, 0, 0, 2)), ((1, 1, 2, 4),), (), (), ())
+NS = (12, 2)
 CE = (2, 0)
 MM0 = 99
 CQ = {1: 0, 3: 1}
-PT = {1: 0, 4: 1}
+PT = {2: 0, 4: 1}
 GE = (1, 1, 1, 1, 1, 1, 1, 1)
-ALT = ((0, 3), (0, 5), (0, 7), (1, 1), (1, 3), (1, 5))
+ALT = ()
 IL = {(0, 0): "0011", (1, 0): "0011", (0, 1): "0111", (1, 1): "0111"}
-DQ = (("t00",), ("t01",), ("t02",), ("t03", "p0"), ("t10",), (), ("t11", "p1"), ("t12", "t13"))
+DQ = (("t00",), ("t01",), ("p0",), ("t10",), ("t11", "p1"), ("t02",), ("t03",), ("t12",))
 
 
 def tile_heatdampedfunctionalmapsofterror_x1_kernel(tc, psi, cmap, lam, phi, dist, out_0, out_1, out_2):
@@ -68,11 +75,12 @@ def tile_heatdampedfunctionalmapsofterror_x1_kernel(tc, psi, cmap, lam, phi, dis
         def load_rows(dst, src, b, n):
             nc.sync.dma_start(out=dst[:, b:b + n, :], in_=src[P * b:P * (b + n), :].rearrange("(b p) k -> p b k", p=P))
 
-        load_rows(psi_sb, psi, 0, 1)
-        load_rows(psi_sb, psi, 1, 1)
-        load_rows(psi_sb, psi, 2, 2)
         load_cm(0, 0)
         load_cm(1, 0)
+        load_rows(psi_sb, psi, 0, 1)
+        load_rows(psi_sb, psi, 1, 1)
+        load_rows(psi_sb, psi, 2, 1)
+        load_rows(psi_sb, psi, 3, 1)
         load_rows(psi_sb, psi, 4, 2)
         load_rows(psi_sb, psi, 6, 2)
         load_cm(0, 1)
@@ -209,7 +217,7 @@ def tile_heatdampedfunctionalmapsofterror_x1_kernel(tc, psi, cmap, lam, phi, dis
             nc.scalar.activation(out=junk[:], in_=sbank[s, h][:], func=ACT.Square, accum_out=acc[:, s, h:h + 1])
 
         def eps(s):
-            nc.vector.tensor_scalar(out=acce[:, s:s + 1], in0=acc[:, s, 0:1], scalar1=1e-6, scalar2=None, op0=ALU.add)
+            nc.gpsimd.tensor_scalar(out=acce[:, s:s + 1], in0=acc[:, s, 0:1], scalar1=1.0, scalar2=1e-6, op0=ALU.mult, op1=ALU.add)
 
         def rsq(s):
             nc.scalar.activation(out=rn[:, s:s + 1], in_=acc[:, s, 1:2], func=ACT.Abs_reciprocal_sqrt, bias=acce[:, s:s + 1])
@@ -222,7 +230,7 @@ def tile_heatdampedfunctionalmapsofterror_x1_kernel(tc, psi, cmap, lam, phi, dis
 
         def a1_turn(s):
             for st in range(2):
-                bank = psum.tile([P, 4, P], F32, name="tr", tag="tr", bufs=2)
+                bank = psum.tile([P, 4, P], F32, name="mm", tag="mm", bufs=5) if s == 7 else psum.tile([P, 4, P], F32, name="tr", tag="tr", bufs=2)
                 for q in range(4):
                     ib = 2 * q + st
                     nc.tensor.transpose(bank[:, q, :], a1[s][:, P * ib:P * ib + P], ident[:])
@@ -250,7 +258,7 @@ def tile_heatdampedfunctionalmapsofterror_x1_kernel(tc, psi, cmap, lam, phi, dis
 
         def e_turn(s, st):
             if st == 0:
-                bank = psum.tile([P, 2, 2, P], F32, name="ew", tag="ew", bufs=1)
+                bank = psum.tile([P, 2, 2, P], F32, name="mm", tag="mm", bufs=5) if s > 5 else psum.tile([P, 2, 2, P], F32, name="ew", tag="ew", bufs=1)
                 ebank[s] = bank
             words = eb[s].rearrange("p s u x e -> p (s u x e)").bitcast(F32)
             for u in range(2):
@@ -281,7 +289,7 @@ def tile_heatdampedfunctionalmapsofterror_x1_kernel(tc, psi, cmap, lam, phi, dis
         def store_words(s, eng):
             g, w0 = s // 4, 32 * (s % 4)
             for q in range(4):
-                (nc.sync if eng == 0 else nc.scalar).dma_start(
+                (nc.scalar if eng == 1 and q > 1 else nc.sync).dma_start(
                     out=o1[g, w0:w0 + 32, 256 * q:256 * q + 256, :].rearrange("w i o -> w (i o)"),
                     in_=pc[s][32 * q:32 * q + 32, :].bitcast(I32))
 
@@ -303,60 +311,67 @@ def tile_heatdampedfunctionalmapsofterror_x1_kernel(tc, psi, cmap, lam, phi, dis
                     il(int(e), kk, g, t, t1)
                 t = max(t1, t + 1)
 
-        spin(5)
-        for b in range(4):
-            turn(psi_sb, "psi", b)
-            spin(1)
-            group(GE[b], "psi", b)
-            if b > 0:
-                quant(psi_c, psi_s, "psi", b - 1)
-        nc.scalar.activation(out=warm[:], in_=damp[:].rearrange("p g t -> p (g t)"), func=ACT.Abs_reciprocal_sqrt)
-        quant(psi_c, psi_s, "psi", 3)
+        spin(NS[0])
         for kk in range(2):
-            for e in "012":
+            for e in "01":
                 il_all(kk, 0, e)
             cm_q(kk, 0)
-        spin(6)
-        for b in range(4, 8):
+        nc.scalar.activation(out=warm[:], in_=damp[:].rearrange("p g t -> p (g t)"), func=ACT.Abs_reciprocal_sqrt)
+        for b in range(2):
             turn(psi_sb, "psi", b)
-            if b % 2 == 1:
-                spin(1)
             group(GE[b], "psi", b)
-            if b > 4:
-                quant(psi_c, psi_s, "psi", b - 1)
-        quant(psi_c, psi_s, "psi", 7)
-        for g in range(2):
-            for b in range(8):
-                st1(g, b)
-                if g == 0 and b in CQ:
-                    kk = CQ[b]
-                    for e in "012":
-                        il_all(kk, 1, e)
-                    cm_q(kk, 1)
-                if g == 1 and b in PT:
-                    turn(phi_sb, "phi", PT[b])
-                    group(1, "phi", PT[b])
-                th(g, b)
-                if (g, b - 1) in ALT:
-                    th_late(g, b - 1)
-                elif g == 1 and b == 0 and (0, 7) in ALT:
-                    th_late(0, 7)
-                if g == 1:
-                    for x in DQ[b]:
-                        if x[0] == "t":
-                            th_q(int(x[1]), int(x[2]))
-                        else:
-                            quant(phi_c, phi_s, "phi", int(x[1]))
-                    if b == MM0:
-                        mm(0, 0)
-                        sq(0, 0)
-                        eps(0)
+            quant(psi_c, psi_s, "psi", b)
+        spin(NS[1])
+        for c in range(4):
+            if c < 3:
+                for b in (2 * c + 2, 2 * c + 3):
+                    if c == 0 and b == 3:
+                        st1(0, 0)
+                    turn(psi_sb, "psi", b)
+                    group(GE[b], "psi", b)
+            for b in (2 * c, 2 * c + 1):
+                if b > 0:
+                    st1(0, b)
+                if b % 2 == 0:
+                    pass
+                    for q in ((b + 2, b + 3) if c < 3 else ()):
+                        quant(psi_c, psi_s, "psi", q)
+                    th(0, b)
+                else:
+                    th(0, b)
+                if (0, b - 1) in ALT:
+                    th_late(0, b - 1)
+                for e, kk, t0, t1 in ILS[b]:
+                    il(e, kk, 1, t0, t1)
+                if b == CMQ[0]:
+                    cm_q(0, 1)
+                if b == CMQ[1]:
+                    cm_q(1, 1)
+        for b in range(8):
+            st1(1, b)
+            if b in PT:
+                turn(phi_sb, "phi", PT[b])
+                group(1, "phi", PT[b])
+            th(1, b)
+            if b > 0 and (1, b - 1) in ALT:
+                th_late(1, b - 1)
+            elif b == 0 and (0, 7) in ALT:
+                th_late(0, 7)
+            for x in DQ[b]:
+                if x[0] == "t":
+                    th_q(int(x[1]), int(x[2]))
+                else:
+                    quant(phi_c, phi_s, "phi", int(x[1]))
+            if b == EM[0]:
+                mm(0, 0)
+                sq(0, 0)
+                eps(0)
+            if b == EM[1]:
+                mm(1, 0)
+                sq(1, 0)
+        th_q(1, 3)
         turn(phi_sb, "phi", 2)
         group(1, "phi", 2)
-        mm(0, 0)
-        mm(1, 0)
-        sq(0, 0)
-        eps(0)
         turn(phi_sb, "phi", 3)
         group(1, "phi", 3)
         mm(0, 1)
@@ -364,22 +379,23 @@ def tile_heatdampedfunctionalmapsofterror_x1_kernel(tc, psi, cmap, lam, phi, dis
         quant(phi_c, phi_s, "phi", 2)
         quant(phi_c, phi_s, "phi", 3)
         sq(0, 1)
-        sq(1, 0)
         rsq(0)
         absn(0, 0)
         absn(0, 1)
         sq(1, 1)
         turn(phi_sb, "phi", 4)
-        group(0, "phi", 4)
+        group(PG[0], "phi", 4)
         turn(phi_sb, "phi", 5)
-        group(0, "phi", 5)
+        group(PG[1], "phi", 5)
         quant(phi_c, phi_s, "phi", 4)
         for s in range(8):
             last = s == 7
             if s < 6:
                 mm(s + 2, 0)
+                if not SPREAD:
+                    mm(s + 2, 1)
             a1_turn(s)
-            if s < 6:
+            if s < 6 and SPREAD:
                 mm(s + 2, 1)
             if s < 2:
                 turn(phi_sb, "phi", 6 + s)
@@ -391,17 +407,21 @@ def tile_heatdampedfunctionalmapsofterror_x1_kernel(tc, psi, cmap, lam, phi, dis
             cast(s, 1 if last else CE[0], 0)
             store(s, 0)
             emul(s, 1)
-            cast(s, 1 if last else CE[1], 1)
-            store(s, 1)
-            if s < 2:
-                group(0, "phi", 6 + s)
-            if s > 1:
-                e_quant(s - 2, 0, 2)
-                store_words(s - 2, 0)
+            if last:
+                cast(s, 1, 1)
+                store(s, 1)
             if s > 0:
                 e_turn(s - 1, 0)
                 e_turn(s - 1, 1)
-                e_group(s - 1, 0, 0, 2)
+                e_group(s - 1, EG[s - 1], 0, 2)
+            if s < 2:
+                group(PG[2 + s], "phi", 6 + s)
+            if not last:
+                cast(s, CE[1], 1)
+                store(s, 1)
+            if s > 0:
+                e_quant(s - 1, 0, 2)
+                store_words(s - 1, 0)
             if s < 6:
                 sq(s + 2, 0)
             if s < 7:
@@ -411,14 +431,12 @@ def tile_heatdampedfunctionalmapsofterror_x1_kernel(tc, psi, cmap, lam, phi, dis
             if s < 6:
                 sq(s + 2, 1)
         e_turn(7, 0)
-        e_quant(6, 0, 2)
-        store_words(6, 0)
         e_turn(7, 1)
         e_group(7, 0, 0, 1)
         e_group(7, 1, 1, 2)
         e_quant(7, 0, 1)
         e_quant(7, 1, 2)
-        store_words(7, 0)
+        store_words(7, 1)
         o2 = out_2.rearrange("g (s q) i -> q (g s) i", q=4).bitcast(I32)
         for q in range(4):
             nc.scalar.dma_start(out=o2[:, :, 64 * q:64 * q + 64], in_=pl_s[32 * q:32 * q + 4, :, :].bitcast(I32))

from contextlib import ExitStack

import concourse.mybir as mybir
from concourse.masks import make_identity

M, K, L, N = 1024, 1024, 1024, 1024
FLOPS = 2 * M * K * L + 2 * M * L * N

F32 = mybir.dt.float32
BF16 = mybir.dt.bfloat16
U32 = mybir.dt.uint32
I32 = mybir.dt.int32
U8 = mybir.dt.uint8
X4 = mybir.dt.float8_e4m3fn_x4
ACT = mybir.ActivationFunctionType
ALU = mybir.AluOpType

P = 128
EM = (6, 7)
PG = (0, 0, 0, 0)
EG = (0, 0, 0, 0, 0, 0, 0)
SPREAD = True
CMQ = (3, 4)
ILS = ((), (), ((1, 0, 2, 4), (0, 1, 0, 1)), ((1, 1, 1, 2), (0, 0, 0, 2)), ((1, 1, 2, 4),), (), (), ())
NS = (12, 2)
CE = (2, 0)
MM0 = 99
CQ = {1: 0, 3: 1}
PT = {2: 0, 4: 1}
GE = (1, 1, 1, 1, 1, 1, 1, 1)
ALT = ()
IL = {(0, 0): "0011", (1, 0): "0011", (0, 1): "0111", (1, 1): "0111"}
DQ = (("t00",), ("t01",), ("p0",), ("t10",), ("t11", "p1"), ("t02",), ("t03",), ("t12",))


def tile_heatdampedfunctionalmapsofterror_x1_kernel(tc, psi, cmap, lam, phi, dist, out_0, out_1, out_2):
    nc = tc.nc
    with ExitStack() as ctx:
        keep = ctx.enter_context(tc.tile_pool(name="keep", bufs=1))
        work = ctx.enter_context(tc.tile_pool(name="work", bufs=2))
        psum = ctx.enter_context(tc.psum_pool(name="psum", bufs=1))
        ctx.enter_context(tc.manual_schedule())

        ident = keep.tile([P, P], F32, name="ident")
        lam_sb = keep.tile([P, 2, 4], BF16, name="lam_sb")
        damp = keep.tile([P, 2, 4], F32, name="damp")
        warm = keep.tile([P, 8], F32, name="warm")

        psi_sb = keep.tile([P, 8, K], BF16, name="psi_sb", align_bytes=64)
        phi_sb = keep.tile([P, 8, L], BF16, name="phi_sb", align_bytes=64)
        dist_sb = keep.tile([P, 2, 4, N], BF16, name="dist_sb", align_bytes=64)
        cm_raw = [keep.tile([P, 4, 512], BF16, name="cm_raw%d" % i, align_bytes=64) for i in range(4)]
        cm_il = [keep.tile([P, 4, 128, 4], BF16, name="cm_il%d" % i, align_bytes=64) for i in range(4)]
        cm_c = [keep.tile([P, 512], U32, name="cm_c%d" % i, align_bytes=64) for i in range(4)]
        cm_s = [keep.tile([P, 512], U8, name="cm_s%d" % i, align_bytes=64) for i in range(4)]
        psi_c = keep.tile([P, 8, 256], U32, name="psi_c", align_bytes=64)
        psi_s = keep.tile([P, 8, 256], U8, name="psi_s", align_bytes=64)
        phi_c = keep.tile([P, 8, 256], U32, name="phi_c", align_bytes=64)
        phi_s = keep.tile([P, 8, 256], U8, name="phi_s", align_bytes=64)
        th_c = keep.tile([P, 2, M], U32, name="th_c", align_bytes=64)
        th_s = keep.tile([P, 2, M], U8, name="th_s", align_bytes=64)
        pl_s = keep.tile([P, 8, 256], U8, name="pl_s", align_bytes=64)
        acc = keep.tile([P, 8, 2], F32, name="acc")
        acce = keep.tile([P, 8], F32, name="acce")
        rn = keep.tile([P, 8], F32, name="rn")

        nc.scalar.dma_start(out=lam_sb[:], in_=lam.rearrange("(g p t) -> p g t", g=2, t=4))

        def load_cm(kk, g):
            nc.sync.dma_start(
                out=cm_raw[2 * kk + g][:],
                in_=cmap[512 * kk:512 * kk + 512, 512 * g:512 * g + 512].rearrange("(p j) l -> p j l", j=4),
            )

        def load_rows(dst, src, b, n):
            nc.sync.dma_start(out=dst[:, b:b + n, :], in_=src[P * b:P * (b + n), :].rearrange("(b p) k -> p b k", p=P))

        load_cm(0, 0)
        load_cm(1, 0)
        load_rows(psi_sb, psi, 0, 1)
        load_rows(psi_sb, psi, 1, 1)
        load_rows(psi_sb, psi, 2, 1)
        load_rows(psi_sb, psi, 3, 1)
        load_rows(psi_sb, psi, 4, 2)
        load_rows(psi_sb, psi, 6, 2)
        load_cm(0, 1)
        load_cm(1, 1)
        for b in range(0, 8, 2):
            load_rows(phi_sb, phi, b, 2)
        dview = dist.rearrange("(q s p) j -> s p q j", q=4, s=2)
        for st in range(2):
            nc.sync.dma_start(out=dist_sb[:, st, :, :], in_=dview[st])

        wz = keep.tile([P, 512], BF16, name="wz", align_bytes=64)
        nc.vector.memset(wz[:], 0.0)
        make_identity(nc, ident[:])
        nc.scalar.activation(out=damp[:], in_=lam_sb[:], func=ACT.Exp, scale=-0.5)

        def il(eng, kk, g, t0, t1):
            i = 2 * kk + g
            dst = cm_il[i][:, t0:t1, :, :]
            src = cm_raw[i].rearrange("p j (m t) -> p t m j", t=4)[:, t0:t1, :, :]
            if eng == 0:
                nc.vector.tensor_copy(out=dst, in_=src)
            elif eng == 1:
                nc.scalar.copy(out=dst, in_=src)
            else:
                nc.gpsimd.tensor_scalar(out=dst, in0=src, scalar1=1.0, scalar2=0.0, op0=ALU.mult, op1=ALU.add)

        def cm_q(kk, g):
            i = 2 * kk + g
            nc.vector.quantize_mx(out=cm_c[i][:].bitcast(X4), scales=cm_s[i][:],
                                  in_=cm_il[i].rearrange("p t m j -> p (t m j)"))

        banks = {}
        grouped = {}

        def spin(n):
            for i in range(n):
                bank = psum.tile([P, 512], F32, name="mm", tag="mm", bufs=5)
                nc.tensor.matmul(bank[:], lhsT=wz[:, 0:P], rhs=wz[:], start=True, stop=True)

        def turn(src, key, b):
            bank = psum.tile([P, 2, 2, P], F32, name="tr", tag="tr", bufs=2)
            words = src[:, b, :].bitcast(F32)
            for kk in range(2):
                for u in range(2):
                    nc.tensor.transpose(bank[:, kk, u, :], words[:, 256 * kk + u:256 * (kk + 1):2], ident[:])
            banks[key, b] = bank

        def group(eng, key, b):
            gr = work.tile([P, 2, P, 4], BF16, name="gr", tag="gr", bufs=4, align_bytes=64)
            dst = gr.rearrange("p k r t -> p (k r t)").bitcast(F32).rearrange("p (k r u) -> p k r u", k=2, u=2)
            src = banks[key, b].rearrange("p k u r -> p k r u")
            if eng == 0:
                nc.vector.tensor_copy(out=dst, in_=src)
            else:
                nc.scalar.copy(out=dst, in_=src)
            grouped[key, b] = gr

        def quant(codes, scales, key, b):
            nc.vector.quantize_mx(out=codes[:, b, :].bitcast(X4), scales=scales[:, b, :],
                                  in_=grouped[key, b].rearrange("p k r t -> p (k r t)"))

        tbank = {}
        thb = {}

        def st1(g, b):
            bank = psum.tile([P, 4, P], F32, name="mm", tag="mm", bufs=5)
            for t in range(4):
                for kk in range(2):
                    i = 2 * kk + g
                    nc.tensor.matmul_mx(
                        out=bank[:, t, :],
                        lhsT=cm_c[i][:, P * t:P * t + P].bitcast(X4), lhsT_scale=cm_s[i][:, P * t:P * t + P],
                        rhs=psi_c[:, b, P * kk:P * kk + P].bitcast(X4), rhs_scale=psi_s[:, b, P * kk:P * kk + P],
                        start=(kk == 0), stop=(kk == 1))
            tbank[g, b] = bank

        def th_mul(g, b):
            c = b // 2
            if b % 2 == 0:
                tht = work.tile([P, 2, P, 4], BF16, name="thb", tag="thb", bufs=8, align_bytes=64)
                thb[g, c] = tht
            nc.vector.tensor_tensor(
                out=thb[g, c][:, b % 2, :, :],
                in0=tbank[g, b].rearrange("p t i -> p i t"),
                in1=damp[:, g, :].unsqueeze(1).to_broadcast([P, P, 4]),
                op=ALU.mult)

        late = {}

        def th_alt(g, b):
            c = b // 2
            if b % 2 == 0:
                tht = work.tile([P, 2, P, 4], BF16, name="thb", tag="thb", bufs=8, align_bytes=64)
                thb[g, c] = tht
            tmp = work.tile([P, 4, P], BF16, name="tmp", tag="tmp", bufs=3, align_bytes=64)
            for t in range(4):
                nc.scalar.activation(out=tmp[:, t, :], in_=tbank[g, b][:, t, :], func=ACT.Copy, scale=damp[:, g, t:t + 1])
            late[g, b] = tmp

        def th_late(g, b):
            nc.vector.tensor_copy(out=thb[g, b // 2][:, b % 2, :, :], in_=late[g, b].rearrange("p t i -> p i t"))

        def th(g, b):
            if (g, b) in ALT:
                th_alt(g, b)
            else:
                th_mul(g, b)

        def th_q(g, c):
            nc.vector.quantize_mx(out=th_c[:, g, 256 * c:256 * c + 256].bitcast(X4), scales=th_s[:, g, 256 * c:256 * c + 256],
                                  in_=thb[g, c].rearrange("p b r t -> p (b r t)"))

        sbank = {}
        a1 = {}
        abank = {}
        ev = {}
        eb = {}
        ebank = {}
        pg = {}
        pc = {}

        def mm(s, h):
            bank = psum.tile([P, 512], F32, name="mm", tag="mm", bufs=5)
            for g in range(2):
                nc.tensor.matmul_mx(
                    out=bank[:],
                    lhsT=phi_c[:, s, P * g:P * g + P].bitcast(X4), lhsT_scale=phi_s[:, s, P * g:P * g + P],
                    rhs=th_c[:, g, 512 * h:512 * h + 512].bitcast(X4), rhs_scale=th_s[:, g, 512 * h:512 * h + 512],
                    start=(g == 0), stop=(g == 1))
            sbank[s, h] = bank

        def sq(s, h):
            junk = work.tile([P, 512], BF16, name="junk", tag="junk", bufs=2)
            nc.scalar.activation(out=junk[:], in_=sbank[s, h][:], func=ACT.Square, accum_out=acc[:, s, h:h + 1])

        def eps(s):
            nc.gpsimd.tensor_scalar(out=acce[:, s:s + 1], in0=acc[:, s, 0:1], scalar1=1.0, scalar2=1e-6, op0=ALU.mult, op1=ALU.add)

        def rsq(s):
            nc.scalar.activation(out=rn[:, s:s + 1], in_=acc[:, s, 1:2], func=ACT.Abs_reciprocal_sqrt, bias=acce[:, s:s + 1])

        def absn(s, h):
            if h == 0:
                a = work.tile([P, M], F32, name="a1", tag="a1", bufs=3)
                a1[s] = a
            nc.scalar.activation(out=a1[s][:, 512 * h:512 * h + 512], in_=sbank[s, h][:], func=ACT.Abs, scale=rn[:, s:s + 1])

        def a1_turn(s):
            for st in range(2):
                bank = psum.tile([P, 4, P], F32, name="mm", tag="mm", bufs=5) if s == 7 else psum.tile([P, 4, P], F32, name="tr", tag="tr", bufs=2)
                for q in range(4):
                    ib = 2 * q + st
                    nc.tensor.transpose(bank[:, q, :], a1[s][:, P * ib:P * ib + P], ident[:])
                abank[s, st] = bank

        def emul(s, st):
            if st == 0:
                e = work.tile([P, 2, 4, P], F32, name="ev", tag="ev", bufs=4)
                ev[s] = e
            nc.vector.tensor_tensor(out=ev[s][:, st, :, :], in0=abank[s, st][:],
                                    in1=dist_sb[:, st, :, P * s:P * s + P], op=ALU.mult)

        def cast(s, eng, st):
            if st == 0:
                e = work.tile([P, 2, 2, P, 2], BF16, name="eb", tag="eb", bufs=4, align_bytes=64)
                eb[s] = e
            src = ev[s][:, st, :, :].rearrange("p q (w u e) -> p (q w) u e", u=2, e=2)
            dst = eb[s][:, st, :, :, :].rearrange("p u x e -> p x u e")
            if eng == 0:
                nc.vector.tensor_copy(out=dst, in_=src)
            elif eng == 1:
                nc.scalar.copy(out=dst, in_=src)
            else:
                nc.gpsimd.tensor_scalar(out=dst, in0=src, scalar1=1.0, scalar2=0.0, op0=ALU.mult, op1=ALU.add)

        def e_turn(s, st):
            if st == 0:
                bank = psum.tile([P, 2, 2, P], F32, name="mm", tag="mm", bufs=5) if s > 5 else psum.tile([P, 2, 2, P], F32, name="ew", tag="ew", bufs=1)
                ebank[s] = bank
            words = eb[s].rearrange("p s u x e -> p (s u x e)").bitcast(F32)
            for u in range(2):
                o = 256 * st + 128 * u
                nc.tensor.transpose(ebank[s][:, st, u, :], words[:, o:o + P], ident[:])

        def e_group(s, eng, st0, st1):
            if st0 == 0:
                gt = work.tile([P, 2, P, 4], BF16, name="pg", tag="pg", bufs=3, align_bytes=64)
                pg[s] = gt
            dst = pg[s].rearrange("p k r t -> p (k r t)").bitcast(F32).rearrange("p (k r u) -> p k r u", k=2, u=2)[:, st0:st1, :, :]
            src = ebank[s].rearrange("p k u r -> p k r u")[:, st0:st1, :, :]
            if eng == 0:
                nc.vector.tensor_copy(out=dst, in_=src)
            else:
                nc.scalar.copy(out=dst, in_=src)

        o1 = out_1.bitcast(I32)

        def e_quant(s, st0, st1):
            if st0 == 0:
                ct = work.tile([P, 256], U32, name="pc", tag="pc", bufs=3, align_bytes=64)
                pc[s] = ct
            lo, hi = P * st0, P * st1
            nc.vector.quantize_mx(out=pc[s][:, lo:hi].bitcast(X4), scales=pl_s[:, s, lo:hi],
                                  in_=pg[s][:, st0:st1, :, :].rearrange("p k r t -> p (k r t)"))

        def store_words(s, eng):
            g, w0 = s // 4, 32 * (s % 4)
            for q in range(4):
                (nc.scalar if eng == 1 and q > 1 else nc.sync).dma_start(
                    out=o1[g, w0:w0 + 32, 256 * q:256 * q + 256, :].rearrange("w i o -> w (i o)"),
                    in_=pc[s][32 * q:32 * q + 32, :].bitcast(I32))

        o0 = out_0.rearrange("(q s p) j -> s p q j", q=4, s=2)

        def store(s, st):
            nc.sync.dma_start(out=o0[st][:, :, P * s:P * s + P], in_=ev[s][:, st, :, :])

        def ilp(kk, g, t):
            il(int(IL[kk, g][t]), kk, g, t, t + 1)

        def il_all(kk, g, e):
            t = 0
            while t < 4:
                t1 = t
                while t1 < 4 and IL[kk, g][t1] == e:
                    t1 += 1
                if t1 > t:
                    il(int(e), kk, g, t, t1)
                t = max(t1, t + 1)

        spin(NS[0])
        for kk in range(2):
            for e in "01":
                il_all(kk, 0, e)
            cm_q(kk, 0)
        nc.scalar.activation(out=warm[:], in_=damp[:].rearrange("p g t -> p (g t)"), func=ACT.Abs_reciprocal_sqrt)
        for b in range(2):
            turn(psi_sb, "psi", b)
            group(GE[b], "psi", b)
            quant(psi_c, psi_s, "psi", b)
        spin(NS[1])
        for c in range(4):
            if c < 3:
                for b in (2 * c + 2, 2 * c + 3):
                    if c == 0 and b == 3:
                        st1(0, 0)
                    turn(psi_sb, "psi", b)
                    group(GE[b], "psi", b)
            for b in (2 * c, 2 * c + 1):
                if b > 0:
                    st1(0, b)
                if b % 2 == 0:
                    pass
                    for q in ((b + 2, b + 3) if c < 3 else ()):
                        quant(psi_c, psi_s, "psi", q)
                    th(0, b)
                else:
                    th(0, b)
                if (0, b - 1) in ALT:
                    th_late(0, b - 1)
                for e, kk, t0, t1 in ILS[b]:
                    il(e, kk, 1, t0, t1)
                if b == CMQ[0]:
                    cm_q(0, 1)
                if b == CMQ[1]:
                    cm_q(1, 1)
        for b in range(8):
            st1(1, b)
            if b in PT:
                turn(phi_sb, "phi", PT[b])
                group(1, "phi", PT[b])
            th(1, b)
            if b > 0 and (1, b - 1) in ALT:
                th_late(1, b - 1)
            elif b == 0 and (0, 7) in ALT:
                th_late(0, 7)
            for x in DQ[b]:
                if x[0] == "t":
                    th_q(int(x[1]), int(x[2]))
                else:
                    quant(phi_c, phi_s, "phi", int(x[1]))
            if b == EM[0]:
                mm(0, 0)
                sq(0, 0)
                eps(0)
            if b == EM[1]:
                mm(1, 0)
                sq(1, 0)
        th_q(1, 3)
        turn(phi_sb, "phi", 2)
        group(1, "phi", 2)
        turn(phi_sb, "phi", 3)
        group(1, "phi", 3)
        mm(0, 1)
        mm(1, 1)
        quant(phi_c, phi_s, "phi", 2)
        quant(phi_c, phi_s, "phi", 3)
        sq(0, 1)
        rsq(0)
        absn(0, 0)
        absn(0, 1)
        sq(1, 1)
        turn(phi_sb, "phi", 4)
        group(PG[0], "phi", 4)
        turn(phi_sb, "phi", 5)
        group(PG[1], "phi", 5)
        quant(phi_c, phi_s, "phi", 4)
        for s in range(8):
            last = s == 7
            if s < 6:
                mm(s + 2, 0)
                if not SPREAD:
                    mm(s + 2, 1)
            a1_turn(s)
            if s < 6 and SPREAD:
                mm(s + 2, 1)
            if s < 2:
                turn(phi_sb, "phi", 6 + s)
            if s < 7:
                eps(s + 1)
            emul(s, 0)
            if s < 3:
                quant(phi_c, phi_s, "phi", 5 + s)
            cast(s, 1 if last else CE[0], 0)
            store(s, 0)
            emul(s, 1)
            if last:
                cast(s, 1, 1)
                store(s, 1)
            if s > 0:
                e_turn(s - 1, 0)
                e_turn(s - 1, 1)
                e_group(s - 1, EG[s - 1], 0, 2)
            if s < 2:
                group(PG[2 + s], "phi", 6 + s)
            if not last:
                cast(s, CE[1], 1)
                store(s, 1)
            if s > 0:
                e_quant(s - 1, 0, 2)
                store_words(s - 1, 0)
            if s < 6:
                sq(s + 2, 0)
            if s < 7:
                rsq(s + 1)
                absn(s + 1, 0)
                absn(s + 1, 1)
            if s < 6:
                sq(s + 2, 1)
        e_turn(7, 0)
        e_turn(7, 1)
        e_group(7, 0, 0, 1)
        e_group(7, 1, 1, 2)
        e_quant(7, 0, 1)
        e_quant(7, 1, 2)
        store_words(7, 1)
        o2 = out_2.rearrange("g (s q) i -> q (g s) i", q=4).bitcast(I32)
        for q in range(4):
            nc.scalar.dma_start(out=o2[:, :, 64 * q:64 * q + 64], in_=pl_s[32 * q:32 * q + 4, :, :].bitcast(I32))
